import numpy as np
import ml_dtypes


def mxq(x, axis, fmt="e4m3"):
    dtype, down = {"e4m3": (ml_dtypes.float8_e4m3fn, 7), "e5m2": (ml_dtypes.float8_e5m2, 14)}[fmt]
    v = np.moveaxis(np.asarray(x, np.float32).astype(ml_dtypes.bfloat16).astype(np.float64), axis, -1)
    blocks = v.reshape(v.shape[:-1] + (-1, 32))
    amax = np.abs(blocks).max(-1, keepdims=True)
    byte = np.maximum(np.where(amax > 0, np.frexp(amax)[1] - 1 + 127, 0) - down, 1)
    scale = np.exp2(byte - 127.0)
    codes = (blocks / scale).astype(np.float32).astype(dtype).astype(np.float64)
    return np.moveaxis((codes * scale).reshape(v.shape), -1, axis)


WIDE = False


def mx_kscale(k):
    if not WIDE:
        return np.ones(k)
    levels = np.array([10, -10, 5, -5, 0])
    if k % 512:
        return np.exp2(np.random.permutation(np.resize(levels, k // 32))).repeat(32)
    a = np.empty((k // 512, 16))
    for p in range(k // 512):
        a[p, :8] = np.random.permutation(np.resize(levels, 8))
        for g in range(8):
            far = levels[np.abs(levels - a[p, g]) >= 10]
            a[p, g + 8] = far[np.random.randint(len(far))]
    return np.exp2(a.ravel()).repeat(32)


def f64(x):
    return np.asarray(x).astype(np.float64)


def striped(idx):
    return np.tile(idx.reshape(-1, 16).T, (8, 1)).astype(np.uint16)


def unstriped(offs):
    return offs[:16].T.reshape(-1).astype(np.int64)


E2M1 = np.array([0.0, 0.5, 1.0, 1.5, 2.0, 3.0, 4.0, 6.0, -0.0, -0.5, -1.0, -1.5, -2.0, -3.0, -4.0, -6.0])


def pack_weight(w, fmt):
    k, n = w.shape
    w = f64(np.asarray(w, np.float32).astype(ml_dtypes.bfloat16)).reshape(k // 32, 32, n)
    amax = np.abs(w).max(1)
    if fmt == "e4m3":
        byte = np.frexp(amax)[1] - 1 + 127 - 7
    else:
        mant, ex = np.frexp(amax / 6.0)
        byte = np.where(mant > 0.5, ex, ex - 1) + 127
    byte = np.clip(np.where(amax > 0, byte, 1), 1, 254)
    scaled = (w * np.exp2(127.0 - byte)[:, None, :]).reshape(k, n).astype(np.float32)
    by_word = np.ascontiguousarray(scaled.reshape(k // 512, 128, 4, n).transpose(0, 1, 3, 2))
    if fmt == "e4m3":
        words = by_word.astype(ml_dtypes.float8_e4m3fn).view(np.uint8)
    else:
        c = by_word.astype(ml_dtypes.float4_e2m1fn).view(np.uint8) & 0xF
        words = (c[..., 0::2] | (c[..., 1::2] << 4)).reshape(k // 512, 128, 2 * n)
    return np.ascontiguousarray(words), np.ascontiguousarray(byte.astype(np.uint8).reshape(k // 512, 16, n))


def unpack_weight(words, scales, fmt):
    g, _, n = scales.shape
    words = np.ascontiguousarray(words).reshape(g, 128, n, -1)
    if fmt == "e4m3":
        vals = words.view(ml_dtypes.float8_e4m3fn).astype(np.float64)
    else:
        nib = np.empty((g, 128, n, 4), np.uint8)
        nib[..., 0::2] = words & 0xF
        nib[..., 1::2] = words >> 4
        vals = E2M1[nib]
    vals = vals * np.repeat(np.exp2(scales.astype(np.float64) - 127.0), 8, axis=1)[..., None]
    return vals.transpose(0, 1, 3, 2).reshape(g * 512, n)


def silu(v):
    return v / (1.0 + np.exp(-np.maximum(v, -700.0)))


K, T, E, C, H, N = 512, 512, 2, 256, 1024, 256


def by_expert(wq, xq):
    return np.concatenate([wq[e].T @ xq[:, e * C:(e + 1) * C] for e in range(E)], axis=1)


def setup_inputs():
    n = np.random.standard_normal
    s = mx_kscale(K)[:, None]
    u = mx_kscale(H)
    w1 = [pack_weight(m, "e2m1") for m in n((E, K, H)) / np.sqrt(K) / s[None]]
    w3 = [pack_weight(m, "e2m1") for m in n((E, K, H)) / np.sqrt(K) / s[None] * u[None, None, :]]
    w2 = [pack_weight(m, "e2m1") for m in n((E, H, N)) / np.sqrt(H) / u[None, :, None]]
    x = pack_weight(n((K, T)) * s, "e4m3")
    return {
        "x_words": x[0],
        "x_scales": x[1],
        "w1_words": np.stack([m[0] for m in w1]),
        "w1_scales": np.stack([m[1] for m in w1]),
        "w3_words": np.stack([m[0] for m in w3]),
        "w3_scales": np.stack([m[1] for m in w3]),
        "w2_words": np.stack([m[0] for m in w2]),
        "w2_scales": np.stack([m[1] for m in w2]),
        "gate": np.tile(np.random.uniform(0.2, 1.0, E * C), (N, 1)).astype(np.float32),
        "offs": striped(np.random.permutation(T)[:E * C]),
        "dst": striped(np.random.permutation(T)[:E * C]),
    }


def reference(x_words, x_scales, w1_words, w1_scales, w3_words, w3_scales, w2_words, w2_scales, gate, offs, dst):
    idx = unstriped(offs)
    w1 = np.stack([unpack_weight(w1_words[e], w1_scales[e], "e2m1") for e in range(E)])
    w3 = np.stack([unpack_weight(w3_words[e], w3_scales[e], "e2m1") for e in range(E)])
    w2 = np.stack([unpack_weight(w2_words[e], w2_scales[e], "e2m1") for e in range(E)])
    xq = unpack_weight(x_words, x_scales, "e4m3")[:, idx]
    h = silu(by_expert(w1, xq))
    h = h * by_expert(w3, xq)
    y = by_expert(w2, mxq(h, 0, "e4m3"))
    out = np.zeros((N, T))
    out[:, unstriped(dst)] = f64(gate) * y
    return out

@@ -1,0 +1,162 @@
+from contextlib import ExitStack
+
+import concourse.mybir as mybir
+from concourse.masks import make_identity
+
+K, T, E, C, H, N = 512, 512, 2, 256, 1024, 256
+FLOPS = 2 * E * C * (2 * K * H + H * N)
+BYTES = 128 * T * 4 + 16 * T + 2 * E * (128 * 2 * H + 16 * H) + E * 2 * (128 * 2 * N + 16 * N) + T * 4 + 2 * 128 * 32 * 2 + N * T * 4
+
+F32 = mybir.dt.float32
+BF16 = mybir.dt.bfloat16
+I32 = mybir.dt.int32
+U32 = mybir.dt.uint32
+U16 = mybir.dt.uint16
+U8 = mybir.dt.uint8
+FP8X4 = mybir.dt.float8_e4m3fn_x4
+FP4X4 = mybir.dt.float4_e2m1fn_x4
+SILU = mybir.ActivationFunctionType.Silu
+COPY = mybir.ActivationFunctionType.Copy
+MULT = mybir.AluOpType.mult
+
+P = 128
+PASS = 512
+BLOCK = 128
+BLOCKS = E * C // BLOCK
+PASSES = H // PASS
+LIST_COLS = BLOCK // 16
+
+
+def tile_moe_two_glu_silu_kernel(
+    tc, x_words, x_scales, w1_words, w1_scales, w3_words, w3_scales, w2_words, w2_scales, gate, offs, dst, out
+):
+    nc = tc.nc
+    with ExitStack() as ctx:
+        keep = ctx.enter_context(tc.tile_pool(name="keep", bufs=1))
+        work = ctx.enter_context(tc.tile_pool(name="work", bufs=3))
+        psum = ctx.enter_context(tc.psum_pool(name="psum", bufs=2))
+
+        offs_t = keep.tile([P, 32], U16, name="offs_t")
+        dst_t = keep.tile([P, 32], U16, name="dst_t")
+        xw = keep.tile([P, T], I32, name="xw", align_bytes=64)
+        xs = keep.tile([P, T], U8, name="xs", align_bytes=64)
+        w1w = [keep.tile([P, 2 * H], U8, name="w1w%d" % e, align_bytes=64) for e in range(E)]
+        w3w = [keep.tile([P, 2 * H], U8, name="w3w%d" % e, align_bytes=64) for e in range(E)]
+        w2w = keep.tile([P, E * PASSES, 2 * N], U8, name="w2w", align_bytes=64)
+        w1s = keep.tile([P, E, H], U8, name="w1s", align_bytes=64)
+        w3s = keep.tile([P, E, H], U8, name="w3s", align_bytes=64)
+        w2s = keep.tile([P, E * PASSES, N], U8, name="w2s", align_bytes=64)
+        gate_t = keep.tile([P, E * C], F32, name="gate_t")
+        ident = keep.tile([P, P], F32, name="ident")
+        out_t = [keep.tile([P, T], F32, name="out_t%d" % r) for r in range(N // P)]
+        tok_w = [keep.tile([P, BLOCK], U32, name="tok_w%d" % b, align_bytes=64) for b in range(BLOCKS)]
+        tok_s = [keep.tile([P, BLOCK], U8, name="tok_s%d" % b, align_bytes=64) for b in range(BLOCKS)]
+
+        def load_scales(queue, plane, rows):
+            for q in range(4):
+                queue.dma_start(out=plane[32 * q : 32 * q + 4].bitcast(I32), in_=rows[4 * q : 4 * q + 4].bitcast(I32))
+
+        nc.gpsimd.memset(xs[:].bitcast(I32), 0)
+        nc.vector.memset(w1s[:].bitcast(I32), 0)
+        nc.gpsimd.memset(w3s[:].bitcast(I32), 0)
+        nc.vector.memset(w2s[:].bitcast(I32), 0)
+
+        nc.sync.dma_start(out=xw[:], in_=x_words[0].rearrange("p t r -> p (t r)").bitcast(I32))
+        nc.sync.dma_start(offs_t[:], offs)
+        nc.sync.dma_start(out=w1w[0][:].bitcast(I32), in_=w1_words[0, 0].bitcast(I32))
+        nc.sync.dma_start(out=w3w[0][:].bitcast(I32), in_=w3_words[0, 0].bitcast(I32))
+        load_scales(nc.sync, xs, x_scales[0])
+        load_scales(nc.sync, w1s, w1_scales.rearrange("e s q i -> q (e s) i"))
+        load_scales(nc.sync, w3s, w3_scales.rearrange("e s q i -> q (e s) i"))
+        nc.sync.dma_start(out=w2w[:].bitcast(I32), in_=w2_words.rearrange("e s p c -> p (e s) c").bitcast(I32))
+        load_scales(nc.sync, w2s, w2_scales.rearrange("e s q n -> q (e s) n"))
+        nc.sync.dma_start(dst_t[:], dst)
+        nc.sync.dma_start(out=gate_t[:], in_=gate[0:P, :])
+        nc.sync.dma_start(out=w1w[1][:].bitcast(I32), in_=w1_words[1, 0].bitcast(I32))
+        nc.sync.dma_start(out=w3w[1][:].bitcast(I32), in_=w3_words[1, 0].bitcast(I32))
+        make_identity(nc, ident[:])
+
+        for b in range(BLOCKS):
+            cols = offs_t[:, b * LIST_COLS : (b + 1) * LIST_COLS]
+            nc.vector.tensor_copy(out=tok_w[b][:], in_=xw[:].bitcast(U32).indirect(cols))
+            nc.vector.tensor_copy(out=tok_s[b][:], in_=xs[:].indirect(cols))
+
+        turned = {}
+        packed = {}
+
+        def first_layer(b, s):
+            e = b * BLOCK // C
+            sums = []
+            for words, scales, name in ((w1w, w1s, "a1"), (w3w, w3s, "a3")):
+                acc = psum.tile([P, PASS], F32, name=name)
+                nc.tensor.matmul_mx(
+                    out=acc[:],
+                    lhsT=tok_w[b][:].bitcast(FP8X4),
+                    lhsT_scale=tok_s[b][:],
+                    rhs=words[e][:, 2 * PASS * s : 2 * PASS * (s + 1)].bitcast(FP4X4),
+                    rhs_scale=scales[:, e, PASS * s : PASS * (s + 1)],
+                    start=True,
+                    stop=True,
+                )
+                sums.append(acc[:].rearrange("c (p u d) -> c u p d", u=2, d=2))
+            act = work.tile([P, PASS], F32, name="act")
+            act_v = act[:].rearrange("c (u p d) -> c u p d", u=2, d=2)
+            nc.scalar.activation(out=act_v, in_=sums[0], func=SILU)
+            hid = work.tile([P, PASS], BF16, name="hid")
+            nc.vector.tensor_tensor(out=hid[:].rearrange("c (u p d) -> c u p d", u=2, d=2), in0=sums[1], in1=act_v, op=MULT)
+            return hid
+
+        def turn(b, s, hid):
+            if s == 0:
+                turned[b] = psum.tile([P, PASSES, 2, BLOCK], F32, name="turned")
+            pairs = hid[:].bitcast(F32)
+            for u in range(2):
+                nc.tensor.transpose(turned[b][:, s, u, :], pairs[:, u * P : (u + 1) * P], ident[:])
+
+        def quantise(b):
+            hid_t = work.tile([P, PASSES, BLOCK, 2], F32, name="hid_t", align_bytes=64)
+            nc.scalar.copy(out=hid_t[:], in_=turned[b][:].rearrange("p s u c -> p s c u"))
+            codes = work.tile([P, PASSES * BLOCK], U32, name="codes", align_bytes=64)
+            plane = work.tile([P, PASSES * BLOCK], U8, name="plane", align_bytes=64)
+            nc.vector.quantize_mx(
+                out=codes[:].bitcast(FP8X4), scales=plane[:], in_=hid_t[:].rearrange("p s c u -> p (s c u)").bitcast(BF16)
+            )
+            packed[b] = (codes, plane)
+
+        def second_layer(b):
+            e = b * BLOCK // C
+            codes, plane = packed[b]
+            y = psum.tile([P, N // P, BLOCK], F32, name="y")
+            for r in range(N // P):
+                for s in range(PASSES):
+                    nc.tensor.matmul_mx(
+                        out=y[:, r, :],
+                        lhsT=w2w[:, e * PASSES + s, 2 * P * r : 2 * P * (r + 1)].bitcast(FP4X4),
+                        lhsT_scale=w2s[:, e * PASSES + s, P * r : P * (r + 1)],
+                        rhs=codes[:, s * BLOCK : (s + 1) * BLOCK].bitcast(FP8X4),
+                        rhs_scale=plane[:, s * BLOCK : (s + 1) * BLOCK],
+                        start=(s == 0),
+                        stop=(s == PASSES - 1),
+                    )
+            gated = work.tile([P, N // P, BLOCK], F32, name="gated")
+            weight = gate_t[:, b * BLOCK : (b + 1) * BLOCK].unsqueeze(1).to_broadcast([P, N // P, BLOCK])
+            nc.vector.tensor_tensor(out=gated[:], in0=y[:], in1=weight, op=MULT)
+            cols = dst_t[:, b * LIST_COLS : (b + 1) * LIST_COLS]
+            nc.vector.tensor_copy(out=out_t[0][:].indirect(cols), in_=gated[:, 0, :])
+            nc.scalar.activation(out=out_t[1][:].indirect(cols), in_=gated[:, 1, :], func=COPY)
+
+        for step in range(BLOCKS + 1):
+            hids = []
+            if step < BLOCKS:
+                hids.append(first_layer(step, 0))
+            if step >= 1:
+                quantise(step - 1)
+            if step < BLOCKS:
+                hids.append(first_layer(step, 1))
+            if step >= 1:
+                second_layer(step - 1)
+            for s, hid in enumerate(hids):
+                turn(step, s, hid)
+
+        nc.sync.dma_start(out=out[0:P, :], in_=out_t[0][:])
+        nc.scalar.dma_start(out=out[P : 2 * P, :], in_=out_t[1][:])

@@ -49,37 +49,38 @@ def tile_moe_two_glu_silu_kernel(
         gate_t = keep.tile([P, E * C], F32, name="gate_t")
         ident = keep.tile([P, P], F32, name="ident")
         out_t = [keep.tile([P, T], F32, name="out_t%d" % r) for r in range(N // P)]
-        tok_w = [keep.tile([P, BLOCK], U32, name="tok_w%d" % b, align_bytes=64) for b in range(BLOCKS)]
-        tok_s = [keep.tile([P, BLOCK], U8, name="tok_s%d" % b, align_bytes=64) for b in range(BLOCKS)]
+        tok_w = keep.tile([P, E * C], U32, name="tok_w", align_bytes=64)
+        tok_s = keep.tile([P, E * C], U8, name="tok_s", align_bytes=64)
 
         def load_scales(queue, plane, rows):
             for q in range(4):
                 queue.dma_start(out=plane[32 * q : 32 * q + 4].bitcast(I32), in_=rows[4 * q : 4 * q + 4].bitcast(I32))
 
-        nc.gpsimd.memset(xs[:].bitcast(I32), 0)
-        nc.vector.memset(w1s[:].bitcast(I32), 0)
-        nc.gpsimd.memset(w3s[:].bitcast(I32), 0)
+        nc.gpsimd.memset(w1s[:].bitcast(I32), 0)
+        nc.vector.memset(w3s[:].bitcast(I32), 0)
         nc.vector.memset(w2s[:].bitcast(I32), 0)
 
         nc.sync.dma_start(out=xw[:], in_=x_words[0].rearrange("p t r -> p (t r)").bitcast(I32))
         nc.sync.dma_start(offs_t[:], offs)
+        x_rows = x_scales[0].bitcast(I32).rearrange("(q r) c -> q r c", r=4)
+        for r in range(4):
+            nc.sync.dma_start(out=xs[r:P:4, :].bitcast(I32), in_=x_rows[:, r : r + 1, :].to_broadcast([4, 8, T // 4]))
         nc.sync.dma_start(out=w1w[0][:].bitcast(I32), in_=w1_words[0, 0].bitcast(I32))
-        nc.sync.dma_start(out=w3w[0][:].bitcast(I32), in_=w3_words[0, 0].bitcast(I32))
-        load_scales(nc.sync, xs, x_scales[0])
         load_scales(nc.sync, w1s, w1_scales.rearrange("e s q i -> q (e s) i"))
+        nc.sync.dma_start(out=w3w[0][:].bitcast(I32), in_=w3_words[0, 0].bitcast(I32))
         load_scales(nc.sync, w3s, w3_scales.rearrange("e s q i -> q (e s) i"))
+        nc.sync.dma_start(out=w1w[1][:].bitcast(I32), in_=w1_words[1, 0].bitcast(I32))
+        nc.sync.dma_start(out=w3w[1][:].bitcast(I32), in_=w3_words[1, 0].bitcast(I32))
         nc.sync.dma_start(out=w2w[:].bitcast(I32), in_=w2_words.rearrange("e s p c -> p (e s) c").bitcast(I32))
         load_scales(nc.sync, w2s, w2_scales.rearrange("e s q n -> q (e s) n"))
         nc.sync.dma_start(dst_t[:], dst)
         nc.sync.dma_start(out=gate_t[:], in_=gate[0:P, :])
-        nc.sync.dma_start(out=w1w[1][:].bitcast(I32), in_=w1_words[1, 0].bitcast(I32))
-        nc.sync.dma_start(out=w3w[1][:].bitcast(I32), in_=w3_words[1, 0].bitcast(I32))
         make_identity(nc, ident[:])
 
-        for b in range(BLOCKS):
-            cols = offs_t[:, b * LIST_COLS : (b + 1) * LIST_COLS]
-            nc.vector.tensor_copy(out=tok_w[b][:], in_=xw[:].bitcast(U32).indirect(cols))
-            nc.vector.tensor_copy(out=tok_s[b][:], in_=xs[:].indirect(cols))
+        for b0, b1 in ((0, 1), (1, 2), (2, 4)):
+            cols = offs_t[:, b0 * LIST_COLS : b1 * LIST_COLS]
+            nc.vector.tensor_copy(out=tok_w[:, b0 * BLOCK : b1 * BLOCK], in_=xw[:].bitcast(U32).indirect(cols))
+            nc.vector.tensor_copy(out=tok_s[:, b0 * BLOCK : b1 * BLOCK], in_=xs[:].indirect(cols))
 
         turned = {}
         packed = {}
@@ -88,11 +89,11 @@ def tile_moe_two_glu_silu_kernel(
             e = b * BLOCK // C
             sums = []
             for words, scales, name in ((w1w, w1s, "a1"), (w3w, w3s, "a3")):
-                acc = psum.tile([P, PASS], F32, name=name)
+                acc = psum.tile([P, PASS], F32, name=name, bufs=3)
                 nc.tensor.matmul_mx(
                     out=acc[:],
-                    lhsT=tok_w[b][:].bitcast(FP8X4),
-                    lhsT_scale=tok_s[b][:],
+                    lhsT=tok_w[:, b * BLOCK : (b + 1) * BLOCK].bitcast(FP8X4),
+                    lhsT_scale=tok_s[:, b * BLOCK : (b + 1) * BLOCK],
                     rhs=words[e][:, 2 * PASS * s : 2 * PASS * (s + 1)].bitcast(FP4X4),
                     rhs_scale=scales[:, e, PASS * s : PASS * (s + 1)],
                     start=True,
@@ -108,7 +109,7 @@ def tile_moe_two_glu_silu_kernel(
 
         def turn(b, s, hid):
             if s == 0:
-                turned[b] = psum.tile([P, PASSES, 2, BLOCK], F32, name="turned")
+                turned[b] = psum.tile([P, PASSES, 2, BLOCK], F32, name="turned", bufs=1)
             pairs = hid[:].bitcast(F32)
             for u in range(2):
                 nc.tensor.transpose(turned[b][:, s, u, :], pairs[:, u * P : (u + 1) * P], ident[:])
@@ -126,7 +127,7 @@ def tile_moe_two_glu_silu_kernel(
         def second_layer(b):
             e = b * BLOCK // C
             codes, plane = packed[b]
-            y = psum.tile([P, N // P, BLOCK], F32, name="y")
+            y = psum.tile([P, N // P, BLOCK], F32, name="y", bufs=1)
             for r in range(N // P):
                 for s in range(PASSES):
                     nc.tensor.matmul_mx(
@@ -146,17 +147,12 @@ def tile_moe_two_glu_silu_kernel(
             nc.scalar.activation(out=out_t[1][:].indirect(cols), in_=gated[:, 1, :], func=COPY)
 
         for step in range(BLOCKS + 1):
-            hids = []
             if step < BLOCKS:
-                hids.append(first_layer(step, 0))
-            if step >= 1:
-                quantise(step - 1)
-            if step < BLOCKS:
-                hids.append(first_layer(step, 1))
+                for s in range(PASSES):
+                    turn(step, s, first_layer(step, s))
+                quantise(step)
             if step >= 1:
                 second_layer(step - 1)
-            for s, hid in enumerate(hids):
-                turn(step, s, hid)
 
         nc.sync.dma_start(out=out[0:P, :], in_=out_t[0][:])
         nc.scalar.dma_start(out=out[P : 2 * P, :], in_=out_t[1][:])

@@ -33,7 +33,7 @@ def tile_moe_two_glu_silu_kernel(
     nc = tc.nc
     with ExitStack() as ctx:
         keep = ctx.enter_context(tc.tile_pool(name="keep", bufs=1))
-        work = ctx.enter_context(tc.tile_pool(name="work", bufs=3))
+        work = ctx.enter_context(tc.tile_pool(name="work", bufs=4))
         psum = ctx.enter_context(tc.psum_pool(name="psum", bufs=2))
 
         offs_t = keep.tile([P, 32], U16, name="offs_t")
@@ -56,15 +56,15 @@ def tile_moe_two_glu_silu_kernel(
             for q in range(4):
                 queue.dma_start(out=plane[32 * q : 32 * q + 4].bitcast(I32), in_=rows[4 * q : 4 * q + 4].bitcast(I32))
 
-        nc.gpsimd.memset(w1s[:].bitcast(I32), 0)
+        nc.vector.memset(w1s[:].bitcast(I32), 0)
         nc.vector.memset(w3s[:].bitcast(I32), 0)
         nc.vector.memset(w2s[:].bitcast(I32), 0)
 
         nc.sync.dma_start(out=xw[:], in_=x_words[0].rearrange("p t r -> p (t r)").bitcast(I32))
         nc.sync.dma_start(offs_t[:], offs)
-        x_rows = x_scales[0].bitcast(I32).rearrange("(q r) c -> q r c", r=4)
-        for r in range(4):
-            nc.sync.dma_start(out=xs[r:P:4, :].bitcast(I32), in_=x_rows[:, r : r + 1, :].to_broadcast([4, 8, T // 4]))
+        for q in range(4):
+            rows = x_scales[0, 4 * q : 4 * q + 4, :].bitcast(I32)
+            nc.sync.dma_start(out=xs[32 * q : 32 * q + 32, :].bitcast(I32), in_=rows.unsqueeze(0).to_broadcast([8, 4, T // 4]))
         nc.sync.dma_start(out=w1w[0][:].bitcast(I32), in_=w1_words[0, 0].bitcast(I32))
         load_scales(nc.sync, w1s, w1_scales.rearrange("e s q i -> q (e s) i"))
         nc.sync.dma_start(out=w3w[0][:].bitcast(I32), in_=w3_words[0, 0].bitcast(I32))
@@ -82,14 +82,15 @@ def tile_moe_two_glu_silu_kernel(
             nc.vector.tensor_copy(out=tok_w[:, b0 * BLOCK : b1 * BLOCK], in_=xw[:].bitcast(U32).indirect(cols))
             nc.vector.tensor_copy(out=tok_s[:, b0 * BLOCK : b1 * BLOCK], in_=xs[:].indirect(cols))
 
+        ring = [psum.tile([P, PASS], F32, name="ring%d" % i, bufs=1) for i in range(5)]
         turned = {}
         packed = {}
 
         def first_layer(b, s):
             e = b * BLOCK // C
             sums = []
-            for words, scales, name in ((w1w, w1s, "a1"), (w3w, w3s, "a3")):
-                acc = psum.tile([P, PASS], F32, name=name, bufs=3)
+            for j, (words, scales) in enumerate(((w1w, w1s), (w3w, w3s))):
+                acc = ring[(2 * (PASSES * b + s) + j) % len(ring)]
                 nc.tensor.matmul_mx(
                     out=acc[:],
                     lhsT=tok_w[:, b * BLOCK : (b + 1) * BLOCK].bitcast(FP8X4),
@@ -103,7 +104,7 @@ def tile_moe_two_glu_silu_kernel(
             act = work.tile([P, PASS], F32, name="act")
             act_v = act[:].rearrange("c (u p d) -> c u p d", u=2, d=2)
             nc.scalar.activation(out=act_v, in_=sums[0], func=SILU)
-            hid = work.tile([P, PASS], BF16, name="hid")
+            hid = work.tile([P, PASS], BF16, name="hid", bufs=8)
             nc.vector.tensor_tensor(out=hid[:].rearrange("c (u p d) -> c u p d", u=2, d=2), in0=sums[1], in1=act_v, op=MULT)
             return hid
 
@@ -127,11 +128,11 @@ def tile_moe_two_glu_silu_kernel(
         def second_layer(b):
             e = b * BLOCK // C
             codes, plane = packed[b]
-            y = psum.tile([P, N // P, BLOCK], F32, name="y", bufs=1)
+            y = [psum.tile([P, BLOCK], F32, name="y%d" % r, bufs=1) for r in range(N // P)]
             for r in range(N // P):
                 for s in range(PASSES):
                     nc.tensor.matmul_mx(
-                        out=y[:, r, :],
+                        out=y[r][:],
                         lhsT=w2w[:, e * PASSES + s, 2 * P * r : 2 * P * (r + 1)].bitcast(FP4X4),
                         lhsT_scale=w2s[:, e * PASSES + s, P * r : P * (r + 1)],
                         rhs=codes[:, s * BLOCK : (s + 1) * BLOCK].bitcast(FP8X4),
@@ -139,20 +140,25 @@ def tile_moe_two_glu_silu_kernel(
                         start=(s == 0),
                         stop=(s == PASSES - 1),
                     )
-            gated = work.tile([P, N // P, BLOCK], F32, name="gated")
-            weight = gate_t[:, b * BLOCK : (b + 1) * BLOCK].unsqueeze(1).to_broadcast([P, N // P, BLOCK])
-            nc.vector.tensor_tensor(out=gated[:], in0=y[:], in1=weight, op=MULT)
+            weight = gate_t[:, b * BLOCK : (b + 1) * BLOCK]
             cols = dst_t[:, b * LIST_COLS : (b + 1) * LIST_COLS]
-            nc.vector.tensor_copy(out=out_t[0][:].indirect(cols), in_=gated[:, 0, :])
-            nc.scalar.activation(out=out_t[1][:].indirect(cols), in_=gated[:, 1, :], func=COPY)
+            plain = work.tile([P, BLOCK], F32, name="plain")
+            nc.scalar.copy(out=plain[:], in_=y[0][:])
+            gated = work.tile([P, BLOCK], F32, name="gated")
+            nc.vector.tensor_tensor(out=gated[:], in0=y[1][:], in1=weight, op=MULT)
+            nc.vector.tensor_tensor(out=out_t[0][:].indirect(cols), in0=plain[:], in1=weight, op=MULT)
+            nc.scalar.activation(out=out_t[1][:].indirect(cols), in_=gated[:], func=COPY)
 
-        for step in range(BLOCKS + 1):
+        hidden = {}
+        for step in range(BLOCKS + 2):
             if step < BLOCKS:
+                hidden[step] = [first_layer(step, s) for s in range(PASSES)]
+            if 0 <= step - 1 < BLOCKS:
                 for s in range(PASSES):
-                    turn(step, s, first_layer(step, s))
-                quantise(step)
-            if step >= 1:
-                second_layer(step - 1)
+                    turn(step - 1, s, hidden[step - 1][s])
+                quantise(step - 1)
+            if step >= 2:
+                second_layer(step - 2)
 
         nc.sync.dma_start(out=out[0:P, :], in_=out_t[0][:])
         nc.scalar.dma_start(out=out[P : 2 * P, :], in_=out_t[1][:])

from contextlib import ExitStack

import concourse.mybir as mybir
from concourse.masks import make_identity

K, T, E, C, H, N = 512, 512, 2, 256, 1024, 256
FLOPS = 2 * E * C * (2 * K * H + H * N)
BYTES = 128 * T * 4 + 16 * T + 2 * E * (128 * 2 * H + 16 * H) + E * 2 * (128 * 2 * N + 16 * N) + T * 4 + 2 * 128 * 32 * 2 + N * T * 4

F32 = mybir.dt.float32
BF16 = mybir.dt.bfloat16
I32 = mybir.dt.int32
U32 = mybir.dt.uint32
U16 = mybir.dt.uint16
U8 = mybir.dt.uint8
FP8X4 = mybir.dt.float8_e4m3fn_x4
FP4X4 = mybir.dt.float4_e2m1fn_x4
SILU = mybir.ActivationFunctionType.Silu
COPY = mybir.ActivationFunctionType.Copy
MULT = mybir.AluOpType.mult

P = 128
PASS = 512
BLOCK = 128
BLOCKS = E * C // BLOCK
PASSES = H // PASS
LIST_COLS = BLOCK // 16


def tile_moe_two_glu_silu_kernel(
    tc, x_words, x_scales, w1_words, w1_scales, w3_words, w3_scales, w2_words, w2_scales, gate, offs, dst, out
):
    nc = tc.nc
    with ExitStack() as ctx:
        keep = ctx.enter_context(tc.tile_pool(name="keep", bufs=1))
        work = ctx.enter_context(tc.tile_pool(name="work", bufs=4))
        psum = ctx.enter_context(tc.psum_pool(name="psum", bufs=2))

        offs_t = keep.tile([P, 32], U16, name="offs_t")
        dst_t = keep.tile([P, 32], U16, name="dst_t")
        xw = keep.tile([P, T], I32, name="xw", align_bytes=64)
        xs = keep.tile([P, T], U8, name="xs", align_bytes=64)
        w1w = [keep.tile([P, 2 * H], U8, name="w1w%d" % e, align_bytes=64) for e in range(E)]
        w3w = [keep.tile([P, 2 * H], U8, name="w3w%d" % e, align_bytes=64) for e in range(E)]
        w2w = keep.tile([P, E * PASSES, 2 * N], U8, name="w2w", align_bytes=64)
        w1s = keep.tile([P, E, H], U8, name="w1s", align_bytes=64)
        w3s = keep.tile([P, E, H], U8, name="w3s", align_bytes=64)
        w2s = keep.tile([P, E * PASSES, N], U8, name="w2s", align_bytes=64)
        gate_t = keep.tile([P, E * C], F32, name="gate_t")
        ident = keep.tile([P, P], F32, name="ident")
        out_t = [keep.tile([P, T], F32, name="out_t%d" % r) for r in range(N // P)]
        tok_w = keep.tile([P, E * C], U32, name="tok_w", align_bytes=64)
        tok_s = keep.tile([P, E * C], U8, name="tok_s", align_bytes=64)

        def load_scales(queue, plane, rows):
            for q in range(4):
                queue.dma_start(out=plane[32 * q : 32 * q + 4].bitcast(I32), in_=rows[4 * q : 4 * q + 4].bitcast(I32))

        nc.vector.memset(w1s[:].bitcast(I32), 0)
        nc.vector.memset(w3s[:].bitcast(I32), 0)
        nc.vector.memset(w2s[:].bitcast(I32), 0)

        nc.sync.dma_start(out=xw[:], in_=x_words[0].rearrange("p t r -> p (t r)").bitcast(I32))
        nc.sync.dma_start(offs_t[:], offs)
        for q in range(4):
            rows = x_scales[0, 4 * q : 4 * q + 4, :].bitcast(I32)
            nc.sync.dma_start(out=xs[32 * q : 32 * q + 32, :].bitcast(I32), in_=rows.unsqueeze(0).to_broadcast([8, 4, T // 4]))
        nc.sync.dma_start(out=w1w[0][:].bitcast(I32), in_=w1_words[0, 0].bitcast(I32))
        load_scales(nc.sync, w1s, w1_scales.rearrange("e s q i -> q (e s) i"))
        nc.sync.dma_start(out=w3w[0][:].bitcast(I32), in_=w3_words[0, 0].bitcast(I32))
        load_scales(nc.sync, w3s, w3_scales.rearrange("e s q i -> q (e s) i"))
        nc.sync.dma_start(out=w1w[1][:].bitcast(I32), in_=w1_words[1, 0].bitcast(I32))
        nc.sync.dma_start(out=w3w[1][:].bitcast(I32), in_=w3_words[1, 0].bitcast(I32))
        nc.sync.dma_start(out=w2w[:].bitcast(I32), in_=w2_words.rearrange("e s p c -> p (e s) c").bitcast(I32))
        load_scales(nc.sync, w2s, w2_scales.rearrange("e s q n -> q (e s) n"))
        nc.sync.dma_start(dst_t[:], dst)
        nc.sync.dma_start(out=gate_t[:], in_=gate[0:P, :])
        make_identity(nc, ident[:])

        for b0, b1 in ((0, 1), (1, 2), (2, 4)):
            cols = offs_t[:, b0 * LIST_COLS : b1 * LIST_COLS]
            nc.vector.tensor_copy(out=tok_w[:, b0 * BLOCK : b1 * BLOCK], in_=xw[:].bitcast(U32).indirect(cols))
            nc.vector.tensor_copy(out=tok_s[:, b0 * BLOCK : b1 * BLOCK], in_=xs[:].indirect(cols))

        ring = [psum.tile([P, PASS], F32, name="ring%d" % i, bufs=1) for i in range(5)]
        turned = {}
        packed = {}

        def first_layer(b, s):
            e = b * BLOCK // C
            sums = []
            for j, (words, scales) in enumerate(((w1w, w1s), (w3w, w3s))):
                acc = ring[(2 * (PASSES * b + s) + j) % len(ring)]
                nc.tensor.matmul_mx(
                    out=acc[:],
                    lhsT=tok_w[:, b * BLOCK : (b + 1) * BLOCK].bitcast(FP8X4),
                    lhsT_scale=tok_s[:, b * BLOCK : (b + 1) * BLOCK],
                    rhs=words[e][:, 2 * PASS * s : 2 * PASS * (s + 1)].bitcast(FP4X4),
                    rhs_scale=scales[:, e, PASS * s : PASS * (s + 1)],
                    start=True,
                    stop=True,
                )
                sums.append(acc[:].rearrange("c (p u d) -> c u p d", u=2, d=2))
            act = work.tile([P, PASS], F32, name="act")
            act_v = act[:].rearrange("c (u p d) -> c u p d", u=2, d=2)
            nc.scalar.activation(out=act_v, in_=sums[0], func=SILU)
            hid = work.tile([P, PASS], BF16, name="hid", bufs=8)
            nc.vector.tensor_tensor(out=hid[:].rearrange("c (u p d) -> c u p d", u=2, d=2), in0=sums[1], in1=act_v, op=MULT)
            return hid

        def turn(b, s, hid):
            if s == 0:
                turned[b] = psum.tile([P, PASSES, 2, BLOCK], F32, name="turned", bufs=1)
            pairs = hid[:].bitcast(F32)
            for u in range(2):
                nc.tensor.transpose(turned[b][:, s, u, :], pairs[:, u * P : (u + 1) * P], ident[:])

        def quantise(b):
            hid_t = work.tile([P, PASSES, BLOCK, 2], F32, name="hid_t", align_bytes=64)
            nc.scalar.copy(out=hid_t[:], in_=turned[b][:].rearrange("p s u c -> p s c u"))
            codes = work.tile([P, PASSES * BLOCK], U32, name="codes", align_bytes=64)
            plane = work.tile([P, PASSES * BLOCK], U8, name="plane", align_bytes=64)
            nc.vector.quantize_mx(
                out=codes[:].bitcast(FP8X4), scales=plane[:], in_=hid_t[:].rearrange("p s c u -> p (s c u)").bitcast(BF16)
            )
            packed[b] = (codes, plane)

        def second_layer(b):
            e = b * BLOCK // C
            codes, plane = packed[b]
            y = [psum.tile([P, BLOCK], F32, name="y%d" % r, bufs=1) for r in range(N // P)]
            for r in range(N // P):
                for s in range(PASSES):
                    nc.tensor.matmul_mx(
                        out=y[r][:],
                        lhsT=w2w[:, e * PASSES + s, 2 * P * r : 2 * P * (r + 1)].bitcast(FP4X4),
                        lhsT_scale=w2s[:, e * PASSES + s, P * r : P * (r + 1)],
                        rhs=codes[:, s * BLOCK : (s + 1) * BLOCK].bitcast(FP8X4),
                        rhs_scale=plane[:, s * BLOCK : (s + 1) * BLOCK],
                        start=(s == 0),
                        stop=(s == PASSES - 1),
                    )
            weight = gate_t[:, b * BLOCK : (b + 1) * BLOCK]
            cols = dst_t[:, b * LIST_COLS : (b + 1) * LIST_COLS]
            plain = work.tile([P, BLOCK], F32, name="plain")
            nc.scalar.copy(out=plain[:], in_=y[0][:])
            gated = work.tile([P, BLOCK], F32, name="gated")
            nc.vector.tensor_tensor(out=gated[:], in0=y[1][:], in1=weight, op=MULT)
            nc.vector.tensor_tensor(out=out_t[0][:].indirect(cols), in0=plain[:], in1=weight, op=MULT)
            nc.scalar.activation(out=out_t[1][:].indirect(cols), in_=gated[:], func=COPY)

        hidden = {}
        for step in range(BLOCKS + 2):
            if step < BLOCKS:
                hidden[step] = [first_layer(step, s) for s in range(PASSES)]
            if 0 <= step - 1 < BLOCKS:
                for s in range(PASSES):
                    turn(step - 1, s, hidden[step - 1][s])
                quantise(step - 1)
            if step >= 2:
                second_layer(step - 2)

        nc.sync.dma_start(out=out[0:P, :], in_=out_t[0][:])
        nc.scalar.dma_start(out=out[P : 2 * P, :], in_=out_t[1][:])
